import numpy as np, ml_dtypes
CORES = [35,38,43,46]
N = 4
BF = ml_dtypes.bfloat16
S, L, RO, WEAR = 4096, 256, 3, 8
def near(rng, home, h):
    q = S // 16
    return np.take_along_axis(np.broadcast_to(home, (N, 8, S)), h * q + rng.integers(0, q, h.shape), 2)
def parts(rng):
    home = np.argsort(rng.random((8, S)), axis=1); hab = np.zeros((8, S), np.int64)
    np.put_along_axis(hab, home, np.broadcast_to(np.arange(S) // (S // 16), (8, S)), 1)
    base = rng.integers(0, 256, (N, 8, 16, 16))
    x = np.clip(np.take_along_axis(base, hab[None, :, None, :], 3) + rng.integers(-60, 61, (N, 8, 16, S)), 0, 255)
    lab = np.argsort(rng.random((N, 8, L)), axis=2); inv = np.argsort(lab, axis=2)
    h = np.broadcast_to((lab % 16)[:, :, None, :], (N, 8, 16, L)).reshape(N, 8, 16 * L)
    m = np.where(rng.random(h.shape) < 0.75, near(rng, home, h), rng.integers(0, S, h.shape)).reshape(N, 8, 16, L)
    h = np.broadcast_to(hab[None, :, None, :], (N, 8, 16, S)).reshape(N, 8, 16 * S)
    nb = np.where(rng.random(h.shape) < 0.6, near(rng, home, h), rng.integers(0, S, h.shape)).reshape(N, 8, 16, S)
    v = hab[None] + 16 * rng.integers(0, L // 16, (N, 8, S))
    own = np.where(rng.random((N, 8, S)) < 0.6, np.take_along_axis(inv, v, 2), rng.integers(0, L, (N, 8, S)))
    return x, nb, m, own, rng.integers(600, 1100, (N, 8))
def pack(x, nb, m, own, th):
    return {"x0": x.reshape(N, 128, S).astype(np.float32).astype(BF), "nb": nb.reshape(N, 128, S).astype(np.int32), "m0": m.reshape(N, 128, L).astype(np.int32),
            "own0": own.reshape(N, 8, S).astype(np.int32), "th": th.reshape(N, 8, 1).astype(np.int32)}
def setup_inputs(rng):
    return pack(*parts(rng))
def setup_inputs_ties(rng):
    x, nb, m, own, th = parts(rng); step = rng.choice(np.array([1, 5, 40]), (N, 8, 1, 1))
    lo = ((256 - 3 * step) * rng.random((N, 8, 1, 1)) * (rng.random((N, 8, 1, 1)) < 0.7)).astype(np.int64)
    x = lo + step * rng.integers(0, 4, x.shape)
    pool = rng.integers(0, S, (N, 8, 3, L)); few = np.take_along_axis(pool, rng.integers(0, 3, m.shape), 2)
    m = np.where(rng.random((N, 8, 1, L)) < 0.7, few, rng.integers(0, S, m.shape))
    th = step[:, :, 0, 0] * rng.integers(14, 19, (N, 8))
    z = int(rng.integers(0, 8)); o = rng.permutation(S); cold, warm = o[:S // 2], o[S // 2:]; h = rng.integers(140, 250, N)
    is_cold = np.zeros(S, bool); is_cold[cold] = True
    x[:, z] = np.where(is_cold, 0, h[:, None, None]) + rng.integers(0, 2, (N, 16, S))
    three = cold[rng.integers(0, S // 2, (N, 3, L))]; m[:, z] = np.take_along_axis(three, rng.integers(0, 3, (N, 16, L)), 1)
    nb[:, z] = warm[rng.integers(0, S - S // 2, (N, 16, S))]; th[:, z] = 16 * h + rng.integers(3, 9, N)
    return pack(x, nb, m, own, th)
def setup_inputs_corners(rng):
    x, nb, m, own, th = parts(rng); K = S // L; ev = (K + 1) // 2; od = K // 2
    q = int(rng.integers(0, N)); p = (q - 1) % N; u = (q - 2) % N; la = np.arange(L); st = np.arange(S)
    turn = [rng.permutation(8) for r in range(N)]; turn[u] = turn[p]
    for r in range(N):
        for i, g in enumerate(turn[r]):
            if i == 0: own[r, g] = int(rng.choice(np.array([0, L - 1, L // 2])))
            if i == 1:
                own[r, g] = rng.permutation(L)[st % L]; m[r, g] = la + L * rng.integers(0, K, (16, L))
            if i == 2: m[r, g] = rng.choice(np.array([0, S - 1, int(rng.integers(0, S))]), (1, L))
            if i == 3: nb[r, g] = st[None, :]
            if i == 4: nb[r, g] = (S - 1) * rng.integers(0, 2, (1, S))
            if i == 5:
                th[r, g] = 0; x[r, g] = rng.integers(0, WEAR + 2, (16, S))
            if i == 6:
                th[r, g] = 4080; own[r, g] = (L - 1) * rng.integers(0, 2, S); m[r, g] = (S - 1) * rng.integers(0, 2, (16, L))
            if i == 7: x[r, g] = int(rng.choice(np.array([0, 7, 255])))
    x[q] = np.where((st // L) % 2 == 0, rng.integers(0, 9, (8, 16, S)), 255 - rng.integers(0, 9, (8, 16, S)))
    x[q] = np.where(st // L == 1, rng.integers(18, 21, (8, 16, S)), x[q])
    nb[q] = rng.integers(0, L, (8, 16, S)) + 2 * L * rng.integers(0, ev, (8, 16, S)); th[q] = 200
    own[q] = np.argsort(rng.random((8, L)), axis=1)[:, st % L]
    m[q] = la + L * (2 * rng.integers(1, od, (8, 16, L)) + 1); m[p] = la + 2 * L * rng.integers(0, ev, (8, 16, L))
    m[u, int(turn[u][0])] = L + la
    return pack(x, nb, m, own, th)
def setup_inputs_ends(rng):
    home = 1 + np.argsort(rng.random((8, S - 3)), axis=1)[:, :L]; homes = np.broadcast_to(home, (N, 8, L))
    c = rng.choice(np.array([0, 1, 8, 15, 16]), (N, 8)); c[0, 0] = 0; c[0, 1] = 16; c[N - 1] = rng.choice(np.array([1, 8, 15]), 8)
    x = 255 * rng.integers(0, 2, (N, 8, 16, S))
    x[..., 0] = 255 * (np.argsort(rng.random((N, 8, 16)), axis=2) < c[:, :, None]); x[..., S - 1] = 255 - x[..., 0]; x[..., S - 2] = 255
    np.put_along_axis(x, np.broadcast_to(home[None, :, None, :], (N, 8, 16, L)), 0, 3)
    nb = (S - 1) * rng.integers(0, 2, (N, 8, 16, S))
    nb = np.where(rng.random(nb.shape) < 0.15, np.take_along_axis(homes, rng.integers(0, L, (N, 8, 16 * S)), 2).reshape(nb.shape), nb)
    side = rng.integers(0, 2, (N, 8, S)); nb[:, :, 15] = (S - 1) * side; nb[:, :, 0] = (S - 1) * (1 - side)
    sig = np.argsort(rng.random((N, 8, L)), axis=2); own = (L - 1) * rng.integers(0, 2, (N, 8, S)); np.put_along_axis(own, homes, sig, 2)
    mix = (S - 1) * rng.integers(0, 2, (N, 8, 16, L)); kind = rng.choice(np.array([0, 1, 2, 3, 3, 3]), (N, 8, 1, L)); kind[N - 2] = 3; kind[N - 1] = rng.integers(0, 2, (8, 1, L))
    place = np.argsort(rng.random((N, 8, 16, L)), axis=2); place[:, :, :, L - 1] = np.array([2, 3, 4, 5, 6, 7, 8, 9, 10, 11, 12, 13, 14, 15, 0, 1])
    two = rng.random((N, 8, 1, L)) < 0.5; two[..., L - 1] = True
    far = np.where((place == 1) | ((place == 2) & two), S - 2, mix)
    keep = np.where((place == 0) | ((place == 3) & two), home[None, :, None, :], far)
    m = np.where(kind == 0, 0, np.where(kind == 1, S - 1, np.where(kind == 2, mix, keep)))
    th = 4080 * rng.integers(0, 2, (N, 8)); th[:, 2] = 0; th[:, 7] = 4080
    i = int(rng.integers(0, 7)); th[N - 1] = 4080; th[N - 1, i] = 0
    g = (i + 1 + int(rng.integers(0, 6))) % 7; a = int(rng.integers(0, L)); nb[N - 1, g, :, home[g, a]] = m[N - 1, g, 0, sig[N - 1, g, a]]
    return pack(x, nb, m, own, th)
def setup_inputs_spread(rng):
    x, nb, m, own, th = parts(rng)
    x = np.minimum(np.exp2(8 * rng.random((N, 8, 1, S))) * rng.random((N, 8, 16, S)) * 1.25, 255.0).astype(np.int64) * (rng.random((N, 8, 1, S)) > 0.0625)
    m = np.minimum((S * rng.random((N, 8, 16, L)) ** (1 + 3 * rng.random((N, 8, 1, L)))).astype(np.int64), S - 1)
    m = np.where(rng.random((N, 8, 1, L)) < 0.5, m, S - 1 - m)
    u = np.minimum((S * rng.random((N, 4, 16, S)) ** 2).astype(np.int64), S - 1); nb[:, 1::2] = u
    own = np.minimum((L * rng.random((N, 8, S)) ** 2).astype(np.int64), L - 1)
    return pack(x, nb, m, own, np.exp2(8 + 3 * rng.random((N, 8))).astype(np.int64))
def check_inputs(d):
    bad = []
    for k, lo, hi in (("x0", 0, 255), ("nb", 0, S - 1), ("m0", 0, S - 1), ("own0", 0, L - 1), ("th", 0, 4080)):
        try:
            v = np.asarray(d[k]).astype(np.float32).astype(np.float64)
            if not np.all((v >= lo) & (v <= hi)): bad.append("range of " + k)
            elif not np.all(v == np.floor(v)): bad.append("whole numbers of " + k)
        except Exception:
            bad.append("form of " + k)
    return bad
def centre(x, m):
    v = np.take_along_axis(x, m.reshape(8, 1, 16 * L), 2).reshape(8, 16, 16, L)
    c = (np.max(v, axis=2) + np.min(v, axis=2)) >> 1
    d = np.add.reduce(np.abs(v - c[:, :, None, :]), axis=1)
    return c, np.argmin(d, axis=1), np.argmax(d, axis=1)
def reference(x0, nb, m0, own0, th):
    X = x0.astype(np.float32).astype(np.int32).reshape(N, 8, 16, S); nbs = nb.astype(np.int64).reshape(N, 8, 16, S)
    M = m0.astype(np.int64).reshape(N, 8, 16, L); O = own0.astype(np.int64).reshape(N, 8, S); T = th.astype(np.int64).reshape(N, 8)
    wins = np.zeros(N, np.int64); lane = np.broadcast_to(np.arange(L), (8, L)); grp = np.broadcast_to(np.arange(8)[:, None], (8, L))
    for t in range(RO):
        res, back = [], []; now = np.zeros(N, np.int64)
        for q in range(N):
            p = (q - 1 - t % (N - 1)) % N
            ci, ki, fi = centre(X[q], M[p]); cr, kr, fr = centre(X[q], M[q])
            s = np.take_along_axis(M[p], ki[:, None, :], 1)[:, 0]
            b = np.take_along_axis(O[q], s, 1)
            low = np.full((8, L), L); np.minimum.at(low, (grp, b), lane)
            fight = np.take_along_axis(low, b, 1) == lane
            n = np.take_along_axis(nbs[q], s[:, None, :], 2)
            v = np.take_along_axis(X[q], n.reshape(8, 1, 16 * L), 2).reshape(8, 16, 16, L)
            ei = np.add.reduce(np.abs(v - ci[:, :, None, :]), axis=1)
            er = np.add.reduce(np.abs(v - np.take_along_axis(cr, b[:, None, :], 2)[:, :, None, :]), axis=1)
            lim = T[q][:, None, None] + (wins[q] & 63)
            won = np.count_nonzero(ei < lim, axis=1) > np.count_nonzero(er < lim, axis=1)
            e = np.where(won[:, None, :], ei, er)
            best = np.take_along_axis(n, np.argmin(e, axis=1)[:, None, :], 1)[:, 0]
            worst = np.take_along_axis(n, np.argmax(e, axis=1)[:, None, :], 1)[:, 0]
            g, a = np.nonzero(fight); w = won[g, a]; bb = b[g, a]; ss = s[g, a]
            res.append((q, g, fr[g, bb], bb, np.where(w, worst[g, a], best[g, a])))
            back.append((p, g, np.where(w, fi[g, a], ki[g, a]), a, np.where(w, best[g, a], worst[g, a])))
            O[q][g, ss] = np.where(w, np.where(bb + 1 == L, 0, bb + 1), bb)
            if t < RO - 1: X[q][g, :, ss] = np.maximum(X[q][g, :, ss] - WEAR, 0)
            now[q] = np.count_nonzero(w)
        for r, g, k, a, z in res + back: M[r][g, k, a] = z
        wins = now
    return {"ym": M.reshape(N, 128, L).astype(np.float32), "yown": O.astype(np.float32)}

@@ -1,0 +1,553 @@
+from concourse.mybir import AluOpType as OP, ActivationFunctionType as AF
+import comms_topo
+
+S, L, RO, WEAR = 4096, 256, 3, 8
+BIG = float(2 ** 26)
+B, F, I, U = "bfloat16", "float32", "int32", "uint16"
+SCRATCH = {"OD": ("dram", [8, S], B)}
+for _d, _l in ((B, "XW:4352 OWN:4352 GR:4096 GI:4096 GN:4096 S1:4096 S2:4096 DI:4096 MX:4096 CR:256 CI:256 CB:256 THB:128 ONE:128 IDB:128 IDN:128 "
+                   "IDH:128 IDC:128 BO:128 MHALF:128 DGA:256 SM1:1024 SM2:1024 ERC:2048 WB:32 WID:32 WIX:32 WIG:32 WER:32 WEX:32 WRD:8 JC:512 LJT:256 LJ:1024 "
+                   "NC:512 SEL:1280 SELR:256 MLO:256 MHI:256 TP:128 RP:128 SCM:256 SC:256 B1:256 KRW:256 KRB:256 OHR:256 EQ:2176 NF:256 FT:256 FAM:512 OHI:256 "
+                   "B0W:256 DBA:256 DB:256 OT:256 XU:256"),
+               (F, "EO:256 ER0:256 ER1:256 ER2:256 TA:1 TB:1 ONF:128 IDF:128 KC:1 CM:256 DG:256 SMF:512 SMA:256 R16:16 AI0:16 ALS:16 ALB:16 "
+                   "KSC:512 KSO:512 KSR:256 EI:1024 EK:1024 SD:256 SS:256 SCR:64 CUM:272 DD:80 SELT:104 TS:64 ERV:256 ERW:512 PW:256 WC:1 M1:256"),
+               (I, "NBW:4096 MI:256 THC:1 TE:1 THI:1 TLO:1 WI:1 WJ:1 NI:256 NJ:256 TT:128 TU:128 RT:128 RU:128 M2:256"),
+               (U, "ML:256 LI0:256 LI1:256 LI2:256 LS:16 LB:16 NL:256 LSD:16 LBD:16")):
+    for _e in _l.split():
+        SCRATCH[_e.split(":")[0]] = ("sbuf", [128, int(_e.split(":")[1])], _d)
+PSUM = ["P%d" % i for i in range(8)]
+for _p in PSUM:
+    SCRATCH[_p] = ("psum", [128, 512], F)
+SEMAPHORES = (["q_v", "q_s", "q_t", "q_g"] + ["d_" + n for n in ("x", "m", "o", "nb", "th", "od", "ow", "ym", "yo")]
+              + [n + str(t) for n in ("al", "ae", "sl", "se") for t in range(RO)])
+
+
+def rank_program(g, core, T, topo):
+    rank = T.rank_of(core)
+    if rank is None:
+        return
+    N = len(T.cores)
+    Q = {"v": g.vector, "s": g.scalar, "t": g.tensor, "g": g, "y": g.sync}
+    done = {n: 0 for n in SEMAPHORES}
+    know = {q: {} for q in Q}
+    clock = {}
+    acc = {}
+
+    def A(name, c0=0, c1=None, st=1, p0=None, p1=None):
+        t = T[name]
+        c1 = t.shape[1] if c1 is None else c1
+        ps = slice(None) if p0 is None else slice(p0, p1)
+        return (t[ps, slice(c0, c1) if st == 1 else slice(c0, c1, st)], [(name, c0, c1)])
+
+    def IND(win, off):
+        return (win[0].indirect(off[0]), win[1] + off[1])
+
+    def ext(t):
+        return (t, [])
+
+    def conflicts(q, reads, writes):
+        need = {}
+        for regs, wr in ((reads, False), (writes, True)):
+            for (b, c0, c1) in regs:
+                for (aq, aw, a0, a1, sem, val) in acc.get(b, []):
+                    if b in PSUM:
+                        if aq == q and (q == "t" or not aw or a1 <= c0 or a0 >= c1):
+                            continue
+                    elif not (aw or wr) or a1 <= c0 or a0 >= c1:
+                        continue
+                    need[sem] = max(need.get(sem, 0), val)
+        return need
+
+    def wait(q, sem, val):
+        if know[q].get(sem, 0) >= val:
+            return
+        Q[q].wait_ge(T.sem[sem], val)
+        for k, v in clock.get((sem, val), {}).items():
+            know[q][k] = max(know[q].get(k, 0), v)
+        know[q][sem] = max(know[q].get(sem, 0), val)
+
+    def note(q, reads, writes, sem, val):
+        for regs, wr in ((writes, True), (reads, False)):
+            for (b, c0, c1) in regs:
+                l = acc.setdefault(b, [])
+                if b in PSUM:
+                    l[:] = [x for x in l if x[0] == q and not (x[2] >= c0 and x[3] <= c1 and (wr or not x[1]))]
+                else:
+                    l[:] = [x for x in l if not (x[2] >= c0 and x[3] <= c1 and (wr or (x[0] == q and not x[1])))]
+                l.append((q, wr, c0, c1, sem, val))
+
+    def waits(q, reads, writes):
+        need = conflicts(q, reads, writes)
+        for s in sorted(need, key=lambda s: -sum(1 for o in need if o != s and clock.get((s, need[s]), {}).get(o, 0) >= need[o])):
+            wait(q, s, need[s])
+
+    def flat(l):
+        return [r for x in l for r in x[1]]
+
+    def emit(q, call, writes, reads, sem=None, n=1):
+        reads, writes = flat(reads), flat(writes)
+        waits(q, reads, writes)
+        sem = sem or "q_" + q
+        done[sem] += n
+        call().then_inc(T.sem[sem], n)
+        clock[(sem, done[sem])] = dict(know[q])
+        note(q if n == 1 else "d" + sem, reads, writes, sem, done[sem])
+
+    def w_emit(q, call, out, reads):
+        emit(q, call, [(None, out[1][:1])], list(reads) + [(None, out[1][1:])])
+
+    def cp(out, i):
+        w_emit("v", lambda: g.vector.tensor_copy(out[0], i[0]), out, [i])
+
+    def tt(out, a, b, op):
+        w_emit("v", lambda: g.vector.tensor_tensor(out[0], a[0], b[0], op), out, [a, b])
+
+    def ts(out, a, s1, op0, s2=None, op1=None):
+        col = [s1] if isinstance(s1, tuple) else []
+        v = s1[0] if col else s1
+        if op1 is None:
+            w_emit("v", lambda: g.vector.tensor_scalar(out[0], a[0], v, None, op0), out, [a] + col)
+        else:
+            w_emit("v", lambda: g.vector.tensor_scalar(out[0], a[0], v, s2, op0, op1), out, [a] + col)
+
+    def scan(out, d0, d1, op0, op1, init=0.0):
+        w_emit("v", lambda: g.vector.tensor_tensor_scan(out[0], d0[0], d1[0], init, op0, op1), out, [d0, d1])
+
+    def fill(out, c):
+        w_emit("v", lambda: g.vector.memset(out[0], c), out, [])
+
+    def act(out, i, func, bias=0.0, scale=1.0, accum=None):
+        emit("s", lambda: g.scalar.activation(out[0], i[0], func, bias=bias, scale=scale, accum_out=accum and accum[0]), [out] + ([accum] if accum else []), [i])
+
+    def mm(out, l, r, start=False, stop=False):
+        emit("t", lambda: g.tensor.matmul(out[0], l[0], r[0], start, stop), [out], [l, r])
+
+    def aff(out, i, pat, op, fl, base, cm):
+        emit("g", lambda: g.affine_select(out[0], i[0], pat, op, fl, base, cm), [out], [i])
+
+    def iota(out, pat, cm):
+        emit("g", lambda: g.iota(out[0], pat, 0, cm, allow_small_or_imprecise_dtypes=True), [out], [])
+
+    def dma(q, out, i, sem):
+        emit(q, lambda: Q[q].dma_start(out[0], i[0]), [out], [i], sem, 16)
+
+    def dmas(q, calls, out, i, sem):
+        waits(q, flat(i), out[1])
+        for call in calls:
+            call().then_inc(T.sem[sem], 16)
+        done[sem] += 16 * len(calls)
+        clock[(sem, done[sem])] = dict(know[q])
+        note("d" + sem, flat(i), out[1], sem, done[sem])
+
+    def lanes(src, dst):
+        return topo.engines(src, dst)[:8]
+
+    def send(dst, out, i, rsem, lsem):
+        rid, pid = topo.addr(dst)[:2]
+        eng = lanes(core, dst)
+        waits("g", i[1], [])
+        g.remote_dma(out[0], i[0], T.sem[rsem], T.sem[lsem], pid, rid, sum(1 << e for e in eng))
+        done[lsem] += len(eng)
+        clock[(lsem, done[lsem])] = dict(know["g"])
+        note("r" + lsem, i[1], [], lsem, done[lsem])
+
+    def arrives(name, rsem, src):
+        done[rsem] += len(lanes(src, core))
+        note("n" + rsem, [], A(name)[1], rsem, done[rsem])
+
+    fill(A("THC"), 0)
+    dma("y", A("XW", 0, S), ext(T.x0[:]), "d_x")
+    dma("s", A("MI"), ext(T.m0[:]), "d_m")
+    dma("s", A("NI"), ext(T.own0[:]), "d_o")
+    dmas("y", [lambda r=r: g.sync.dma_start(T.THC[r::16, 0:1], T.th[:]) for r in range(2)], A("THC"), [], "d_th")
+    dma("y", A("NBW"), ext(T.nb[:]), "d_nb")
+    fill(A("ONE"), 1.0)
+    iota(A("CM"), [[0, 16], [1, 16]], 0)
+    iota(A("WI"), [[0, 1]], 1)
+    aff(A("IDB"), A("ONE"), [[-1, 128]], OP.is_equal, 0.0, 0, 1)
+    aff(A("WB"), A("ONE", 0, 32), [[0, 4], [-16, 8]], OP.is_ge, 0.0, 0, 1)
+    aff(A("WB"), A("WB"), [[0, 4], [16, 8]], OP.is_ge, 0.0, 15, -1)
+    aff(A("BO"), A("ONE"), [[-16, 8], [0, 16]], OP.is_ge, 0.0, 0, 1)
+    aff(A("BO"), A("BO"), [[16, 8], [0, 16]], OP.is_ge, 0.0, 15, -1)
+    iota(A("AI0"), [[16, 16]], 0)
+    fill(A("MHALF"), -0.5)
+    ts(A("SM1", 0, 256), A("CM"), 0.0, OP.not_equal)
+    ts(A("SM2", 0, 256), A("CM"), 0.0, OP.is_equal, 1024.0, OP.mult)
+    for c in (256, 512):
+        for n in ("SM1", "SM2"):
+            cp(A(n, c, 2 * c), A(n, 0, c))
+    ts(A("WJ"), A("WI"), 15, OP.bitwise_and)
+    ts(A("IDH"), A("IDB"), 0.5, OP.mult)
+    cp(A("KC"), A("WJ"))
+    cp(A("ML"), A("MI"))
+    arrives("LI0", "al0", T.cores[(rank - 1) % N])
+    send(T.cores[(rank + 1) % N], A("LI0"), A("ML"), "al0", "sl0")
+    cp(A("CB"), A("NI"))
+    dma("y", (T.OD[:], [("OD", 0, S)]), A("CB"), "d_od")
+    dmas("y", [lambda r=r: g.sync.dma_start(T.OWN[r::16, 0:S], T.OD[:]) for r in range(16)], A("OWN", 0, S), [("", [("OD", 0, S)])], "d_ow")
+    ts(A("IDN"), A("IDB"), -1.0, OP.mult)
+    ts(A("WID", 0, 16), A("WB", 0, 16), 1024.0, OP.mult)
+    ts(A("WID", 16, 24), A("WB", 0, 8), -64.0, OP.mult)
+    ts(A("WID", 24, 32), A("WB", 0, 8), 64.0, OP.mult)
+    ts(A("WER", 0, 16), A("WB", 0, 16), -1024.0, OP.mult)
+    ts(A("WER", 16, 32), A("WB", 0, 16), 1024.0, OP.mult)
+    ts(A("WRD"), A("WB", 0, 8), -64.0, OP.mult)
+    ts(A("WIX"), A("WID"), 2.0, OP.mult)
+    ts(A("WIG"), A("WID"), -1.0, OP.mult)
+    ts(A("WEX"), A("WER"), -2.0, OP.mult)
+    fill(A("SEL"), 0.0)
+    fill(A("SELR"), 0.0)
+    ts(A("R16"), A("CM", 0, 16), A("KC"), OP.is_equal)
+    ts(A("LJT", 0, 128), A("CM", 0, 128), A("R16", 0, 1), OP.mult)
+    aff(A("LJT", 0, 128), A("LJT", 0, 128), [[0, 128]], OP.is_equal, 0.0, 0, 1)
+    ts(A("SMF", 0, 256), A("CM"), 0.0, OP.is_equal, BIG, OP.mult)
+    ts(A("SMA"), A("CM"), 0.0, OP.not_equal)
+    ts(A("DG"), A("CM"), A("KC"), OP.is_equal)
+    fill(A("ERW"), 0.0)
+
+    def late_constants():
+        ts(A("JC", 0, 128), A("LJT", 0, 128), 64.0, OP.mult)
+        ts(A("JC", 128, 256), A("LJT", 0, 128), 64.0, OP.mult)
+        cp(A("JC", 256, 384), A("LJT", 0, 128))
+        cp(A("JC", 384, 512), A("LJT", 0, 128))
+        cp(A("IDF"), A("IDB"))
+        ts(A("DGA"), A("DG"), 1001.0, OP.mult, -1000.0, OP.add)
+
+        def sel(name, i, row, weight):
+            o = A(name, 128 * i, 128 * i + 128)
+            aff(o, o, [[-1, 8], [0, 16]], OP.not_equal, weight, -row, 1)
+        for h in range(2):
+            sel("SEL", h, 16 * h, 1.0)
+            sel("SEL", h, 16 * h + 8, 64.0)
+        for h in range(2):
+            sel("SEL", 2 + h, 64 + 8 * h, 1.0)
+            sel("SEL", 4 + h, 80 + 8 * h, 1.0)
+            sel("SEL", 6 + h, 32 * h, 1.0)
+            sel("SEL", 6 + h, 32 * h + 8, 64.0)
+            sel("SEL", 8 + h, 32 * h + 16, 1.0)
+            sel("SEL", 8 + h, 32 * h + 24, 64.0)
+            for i, c in ((6, 8192.0), (8, 4096.0)):
+                o = A("SEL", 128 * (i + h), 128 * (i + h) + 128)
+                aff(o, o, [[0, 128]], OP.not_equal, c, -96, 1)
+            sel("SELR", h, 8 * h, 1.0)
+
+    def later_constants():
+        ts(A("ALS"), A("AI0"), A("KC"), OP.add, float(S), OP.add)
+        ts(A("ALB"), A("AI0"), A("KC"), OP.add, float(L + 1), OP.add)
+        for r in range(16):
+            ts(A("ERC", 128 * r, 128 * r + 128), A("IDB"), A("R16", r, r + 1), OP.mult)
+        ts(A("LJT", 0, 128), A("CM", 0, 128), A("R16", 2, 3), OP.mult, 64.0, OP.mult)
+        aff(A("LJT", 0, 128), A("LJT", 0, 128), [[0, 128]], OP.is_equal, 0.0, -2, 1)
+        ts(A("LJT", 128, 256), A("BO"), A("R16", 1, 2), OP.mult, -1024.0, OP.mult)
+        for i in range(2):
+            ts(A("NC", 128 * i, 128 * i + 128), A("BO"), -1024.0, OP.mult)
+            ts(A("NC", 128 * i + 256, 128 * i + 384), A("BO"), 1024.0, OP.mult)
+        ts(A("IDC"), A("IDB"), 100.0, OP.mult)
+        fill(A("ONF"), 1.0)
+        fill(A("XW", S, S + L), 0.0)
+        fill(A("OWN", S, S + L), 0.0)
+        fill(A("CUM", 0, 16), 0.0)
+        fill(A("SELT"), 1.0)
+        tt(A("LJT", 128, 256), A("LJT", 128, 256), A("LJT", 0, 128), OP.add)
+        for i in range(8):
+            c = 128 * i
+            if i in (0, 6):
+                ts(A("LJ", c, c + 128), A("BO"), A("R16", 0, 1), OP.mult, -65536.0, OP.mult)
+                tt(A("LJ", c, c + 128), A("LJ", c, c + 128), A("LJT", 128, 256), OP.add)
+            else:
+                cp(A("LJ", c, c + 128), A("LJT", 0, 128))
+        cp(A("SMF", 256, 512), A("SMF", 0, 256))
+
+    later = []
+
+    def some(n):
+        for _ in range(min(n, len(later))):
+            later.pop(0)()
+
+    def limits(first):
+        if first:
+            later.append(lambda: cp(A("TE"), A("THC")))
+        else:
+            later.append(lambda: cp(A("WI"), A("P3", 0, 1)))
+            later.append(lambda: ts(A("WJ"), A("WI"), 4, OP.logical_shift_right, 63, OP.bitwise_and))
+            later.append(lambda: tt(A("TE"), A("THC"), A("WJ"), OP.add))
+        later.append(lambda: ts(A("THI"), A("TE"), 6, OP.logical_shift_right))
+        later.append(lambda: ts(A("TLO"), A("TE"), 63, OP.bitwise_and))
+        later.append(lambda: tt(A("TA"), A("THI"), A("R16", 0, 1), OP.mult))
+        later.append(lambda: tt(A("TB"), A("TLO"), A("R16", 1, 2), OP.mult))
+        later.append(lambda: tt(A("TA"), A("TA"), A("TB"), OP.add))
+        later.append(lambda: tt(A("TB"), A("TA"), A("R16", 2, 3), OP.add))
+        later.append(lambda: ts(A("THB"), A("ONE"), A("TB"), OP.mult))
+
+    def six(lst):
+        later.append(lambda: cp(A("NI"), A(lst)))
+        later.append(lambda: ts(A("NJ"), A("NI"), 63, OP.bitwise_and))
+        later.append(lambda: ts(A("M2"), A("NI"), 6, OP.logical_shift_right))
+        later.append(lambda: cp(A("MLO"), A("NJ")))
+        later.append(lambda: cp(A("MHI"), A("M2")))
+
+    def gather(q, dst, lst, c):
+        out, src = A(dst, 1024 * c, 1024 * c + 1024), IND(A("XW", 0, S), A(lst, 64 * c, 64 * c + 64))
+        if q == "v":
+            cp(out, src)
+        else:
+            act(out, src, AF.Copy)
+
+    def scans(src, c, n=0):
+        o = 1024 * c
+        scan(A("S1", o, o + 1024), A("SM1"), A(src, o, o + 1024), OP.mult, OP.max)
+        some(n)
+        scan(A("S2", o, o + 1024), A("SM2"), A(src, o, o + 1024), OP.add, OP.min, BIG)
+        some(n)
+
+    def centre(dst, a0, n):
+        for a in range(a0, a0 + n, 128):
+            p = A("P2", a - a0, a - a0 + 128)
+            mm(p, A("IDH"), A("S1", 16 * a + 15, 16 * a + 2048, 16), True, False)
+            mm(p, A("IDH"), A("S2", 16 * a + 15, 16 * a + 2048, 16))
+            mm(p, A("IDH"), A("MHALF"), False, True)
+        ts(A(dst, a0, a0 + n), A("P2", 0, n), float(2 ** 23), OP.add, -float(2 ** 23), OP.add)
+
+    turn = [0]
+
+    def diff(src, cen, h, b, banks):
+        bank = banks[turn[0] % len(banks)]
+        turn[0] += 1
+        for k in range(4):
+            o = A(bank, 128 * k, 128 * k + 128)
+            mm(o, A("IDB"), A(src, 2048 * h + 4 * b + k, 2048 * (h + 1), 16), True, False)
+            mm(o, A("IDN"), A(cen, 128 * h, 128 * h + 128), False, True)
+        act(A("DI", 2048 * h + 512 * b, 2048 * h + 512 * b + 512), A(bank), AF.Abs)
+
+    def sum_d(bank, h, b, w, n=32):
+        for k in range(4 * b, 4 * b + 4):
+            mm(A(bank, k, 16 * n, 16), A("DI", 2048 * h + 128 * k, 2048 * h + 128 * k + 128), A(w), False, k == 15)
+
+    def sum_g(bank, src, h, w):
+        for k in range(16):
+            mm(A(bank, k, 512, 16), A(src, 2048 * h + k, 2048 * (h + 1), 16), A(w))
+
+    def sum_x(bank, h, k, w):
+        mm(A(bank, k, 512, 16), A("MX", 256 * k + 128 * h, 256 * k + 128 * h + 128), A(w), False, k == 15)
+
+    def turned(n, bank, src):
+        o = A(bank, 0, 128, 1, 0, n)
+        emit("t", lambda: g.tensor.transpose(o[0], src[0], A("IDF")[0]), [o], [src, A("IDF")])
+
+    def low(n, bank, mask, x="T"):
+        cp(A(x + "T", 0, 128, 1, 0, n), A(bank, 0, 128, 1, 0, n))
+        ts(A(x + "U", 0, 128, 1, 0, n), A(x + "T", 0, 128, 1, 0, n), mask, OP.bitwise_and)
+        cp(A(x + "P", 0, 128, 1, 0, n), A(x + "U", 0, 128, 1, 0, n))
+
+    def spread(bank, o, name, i, n, start=True, x="TP"):
+        for h in range(2):
+            mm(A(bank, o + 128 * h, o + 128 * h + 128), A(name, 128 * (i + h), 128 * (i + h) + 128, 1, 0, n), A(x, 0, 128, 1, 0, n), start, start or h == 1)
+
+    off = [256 + sum(240 - 16 * d for d in range(c)) for c in range(15)]
+
+    def same(c0, c1):
+        for c in range(c0, c1):
+            some(1)
+            if c == 0:
+                tt(A("EQ", 0, 256), A("SC"), A("B1"), OP.is_equal)
+            else:
+                n = 256 - 16 * c
+                ts(A("EQ", off[c - 1], off[c - 1] + n), A("B1", 256 - n, 256), A("SC", 16 * c - 1, 16 * c), OP.is_equal)
+        some(9)
+
+    THREE, TWO = ["P0", "P1", "P6"], ["P0", "P1"]
+    seq = [(h, b) for h in range(2) for b in range(4)]
+    for t in range(RO):
+        host = T.cores[(rank + 1 + t) % N]
+        guest = T.cores[(rank - 1 - t) % N]
+        LI = "LI%d" % t
+        turn[0] = 0
+        for c in range(4):
+            gather("v" if t == 0 and c == 1 else "s", "GR", "ML", c)
+            if t > 0 and c == 1:
+                act(A("SD"), A("PW"), AF.Copy, accum=A("WC"))
+                mm(A("P3", 0, 1), A("ONF"), A("WC"), True, True)
+        for c in range(4):
+            gather("s", "GI", LI, c)
+        for c in (1, 0, 2, 3) if t == 0 else range(4):
+            scans("GR", c, 3)
+            if c == 0:
+                if t == 0:
+                    late_constants()
+                limits(t == 0)
+                six(LI)
+        some(99)
+        centre("CR", 0, 256)
+        scans("GI", 0)
+        scans("GI", 1)
+        centre("CI", 0, 128)
+        for h in range(2):
+            mm(A(PSUM[3 + h]), A("ONE"), A("JC"), True, False)
+            mm(A(PSUM[3 + h], 0, 128), A("MLO", 128 * h, 128 * h + 128), A("IDB"))
+            mm(A(PSUM[3 + h], 128, 256), A("MHI", 128 * h, 128 * h + 128), A("IDB"))
+        scans("GI", 2)
+        scans("GI", 3)
+        diff("GI", "CI", 0, 0, THREE)
+        diff("GI", "CI", 0, 1, THREE)
+        diff("GI", "CI", 0, 2, THREE)
+        centre("CI", 128, 128)
+        mm(A("P7", 0, 128), A("IDB"), A("CI", 128, 256), True, True)
+        diff("GI", "CI", 0, 3, THREE)
+        sum_g("P4", "GI", 1, "WIG")
+        for k in range(16):
+            tt(A("MX", 256 * k + 128, 256 * k + 256), A("GI", 2048 + k, 4096, 16), A("P7", 0, 128), OP.max)
+        for b in range(4):
+            sum_d("P3", 0, b, "WID")
+            for k in range(4 * b, 4 * b + 4):
+                sum_x("P4", 1, k, "WIX")
+        for h in range(2):
+            scan(A("KSC", 256 * h, 256 * h + 256), A("SMF", 0, 256), A(PSUM[3 + h], 0, 256), OP.add, OP.min, BIG)
+        diff("GR", "CR", 0, 0, THREE)
+        turned(32, "P2", A("KSC", 15, 512, 16))
+        low(32, "P2", 63)
+        diff("GR", "CR", 0, 1, THREE)
+        spread("P2", 0, "SEL", 0, 32)
+        diff("GR", "CR", 0, 2, THREE)
+        tt(A("SD"), A("P2", 0, 256), A("DG"), OP.mult)
+        scan(A("SS"), A("SMA"), A("SD"), OP.mult, OP.add)
+        cp(A("LS"), A("SS", 15, 256, 16))
+        cp(A("NL"), IND(A("NBW"), A("LS")))
+        mm(A("P5", 0, 128), A("ONE"), A("JC", 256, 384), True, False)
+        sum_d("P5", 0, 0, "WRD", 8)
+        diff("GR", "CR", 0, 3, THREE)
+        for b in range(1, 4):
+            sum_d("P5", 0, b, "WRD", 8)
+        for c in range(4):
+            gather("s", "GN", "NL", c)
+        tt(A("SCM"), IND(A("OWN", 0, S), A("LS")), A("DGA"), OP.add)
+        ts(A("B1"), IND(A("OWN", 0, S), A("LS")), 1.0, OP.add)
+        scan(A("KSO", 0, 256), A("SMF", 0, 256), A("P3", 256, 512), OP.add, OP.min, BIG)
+        scan(A("SC"), A("SM1", 0, 256), A("SCM"), OP.mult, OP.max)
+        scan(A("KSO", 256, 512), A("SMF", 0, 256), A("P4", 256, 512), OP.add, OP.min, BIG)
+        ts(A("LB"), A("SC", 15, 256, 16), -1.0, OP.add)
+        scan(A("KSR", 0, 128), A("SMF", 0, 128), A("P5", 0, 128), OP.add, OP.min, BIG)
+        cp(A("CB"), IND(A("CR"), A("LB")))
+        mm(A("P7", 256, 512), A("IDB"), A("CI"), True, True)
+        if t == 0:
+            later_constants()
+        for i in range(4):
+            mm(A(PSUM[3 + i]), A("THB"), A("LJ", 512 * (i // 2), 512 * (i // 2) + 512), True, False)
+            if i < 2:
+                mm(A(PSUM[3 + i]), A("CI", 128 * i, 128 * i + 128), A("NC"))
+        six("NL")
+        same(0, 4)
+        for i in range(4):
+            for j in range(4):
+                mm(A(PSUM[3 + i], 128 * j, 128 * j + 128), A("MHI" if j % 2 else "MLO", 128 * (i % 2), 128 * (i % 2) + 128), A("IDB"))
+        diff("GN", "CB", 0, 0, TWO)
+        diff("GN", "CB", 0, 1, TWO)
+        sum_g("P3", "GN", 0, "WER")
+        same(4, 16)
+        mm(A("P2", 0, 256), A("BO"), A("EQ", 0, 256), True, False)
+        for c in range(15):
+            n = 240 - 16 * c
+            mm(A("P2", 256 - n, 256), A("BO"), A("EQ", off[c], off[c] + n), False, c == 14)
+        for h in range(2):
+            tt(A("DD", 64 + 8 * h, 72 + 8 * h), A("KSO", 256 * h + 15, 256 * h + 128, 16), A("KSO", 256 * h + 143, 256 * h + 256, 16), OP.subtract)
+        ts(A("DBA"), A("B1"), 256.0, OP.is_equal, -256.0, OP.mult)
+        for i, (h, b) in enumerate(seq):
+            if i == 1:
+                sum_g("P4", "GN", 1, "WER")
+            if 0 < i < 7:
+                diff("GN", "CB", seq[i + 1][0], seq[i + 1][1], TWO)
+            for k in (2 * i, 2 * i + 1):
+                tt(A("MX", 256 * k, 256 * k + 256), A("GN", k, 16 * L, 16), A("P7", 256, 512), OP.max)
+                for hh in range(2):
+                    sum_x(PSUM[3 + hh], hh, k, "WEX")
+            sum_d(PSUM[5 + h], h, b, "WER")
+            if i == 3:
+                ts(A("NF"), A("P2", 0, 256), 1.5, OP.is_gt)
+            if i == 5:
+                for r in range(16):
+                    mm(A("P2", 256, 272), A("ERC", 128 * r, 128 * r + 128), A("NF", r, 256, 16), r == 0, r == 15)
+        tt(A("SCR", 0, 16), A("ALS"), A("SS", 15, 256, 16), OP.subtract)
+        tt(A("SCR", 32, 48), A("ALB"), A("SC", 15, 256, 16), OP.subtract)
+        tt(A("SCR", 16, 32), A("SCR", 0, 16), A("P2", 256, 272), OP.mult)
+        tt(A("SCR", 48, 64), A("SCR", 32, 48), A("P2", 256, 272), OP.mult)
+        tt(A("SCR", 0, 16), A("SCR", 16, 32), A("SS", 15, 256, 16), OP.add)
+        tt(A("SCR", 32, 48), A("SCR", 48, 64), A("SC", 15, 256, 16), OP.add)
+        cp(A("LSD"), A("SCR", 0, 16))
+        ts(A("LBD"), A("SCR", 32, 48), -1.0, OP.add)
+        if t < RO - 1:
+            ts(A("XU"), IND(A("XW"), A("LSD")), -float(WEAR), OP.add, 0.0, OP.max)
+
+        def fam(o, bank, c):
+            act(A("FAM", o, o + 128), A(bank, c, c + 128), AF.Sign, -0.5, -1.0)
+
+        def key(out, h, bank):
+            scan(A(out, 512 * h, 512 * h + 512), A("SMF"), A(bank), OP.add, OP.min, BIG)
+        fam(128, "P4", 0)
+        key("EI", 0, "P3")
+        fam(0, "P3", 0)
+        key("EI", 1, "P4")
+        fam(384, "P6", 256)
+        key("EK", 0, "P5")
+        fam(256, "P5", 256)
+        key("EK", 1, "P6")
+        mm(A("P7", 0, 128), A("ONE"), A("JC", 256, 384), True, False)
+        for b in range(4):
+            diff("GR", "CR", 1, b, TWO)
+        for b in range(4):
+            sum_d("P7", 1, b, "WRD", 8)
+        act(A("B0W"), A("B1"), AF.Identity, -1.0)
+        act(A("DB"), A("DBA"), AF.Identity, 1.0)
+        act(A("FT"), A("NF"), AF.Identity, 1.0, -1.0)
+        tt(A("DD", 0, 64), A("EI", 15, 1024, 16), A("EK", 15, 1024, 16), OP.subtract)
+        scan(A("CUM", 16, 272), A("FAM", 0, 256), A("FAM", 256, 512), OP.add, OP.subtract)
+        tt(A("SELT", 80, 96), A("CUM", 31, 272, 16), A("CUM", 15, 256, 16), OP.is_gt)
+        for h in range(2):
+            for c in range(32 * h, 32 * h + 32, 8):
+                tt(A("TS", c, c + 8), A("DD", c, c + 8), A("SELT", 80 + 8 * h, 88 + 8 * h), OP.mult)
+        tt(A("DD", 64, 80), A("DD", 64, 80), A("SELT", 80, 96), OP.mult)
+        tt(A("SELT", 0, 64), A("TS"), A("EK", 15, 1024, 16), OP.add)
+        for h in range(2):
+            tt(A("SELT", 64 + 8 * h, 72 + 8 * h), A("DD", 64 + 8 * h, 72 + 8 * h), A("KSO", 256 * h + 143, 256 * h + 256, 16), OP.add)
+        turned(97, "P2", A("SELT", 0, 97))
+        scan(A("KSR", 128, 256), A("SMF", 0, 128), A("P7", 0, 128), OP.add, OP.min, BIG)
+        turned(16, "P4", A("KSR", 15, 256, 16))
+        low(97, "P2", 63)
+        low(16, "P4", 15, "R")
+        mm(A("P0", 0, 256), A("IDC"), A("NF"), True, False)
+        spread("P0", 0, "SEL", 2, 97, False)
+        spread("P0", 256, "SEL", 6, 97)
+        spread("P1", 0, "SEL", 8, 97)
+        spread("P1", 256, "SEL", 4, 97)
+        ts(A("OHI"), A("P0", 0, 256), A("KC"), OP.is_equal)
+        tt(A("EO"), A("OHI"), A("P0", 256, 512), OP.mult)
+        arrives("ER%d" % t, "ae%d" % t, host)
+        send(guest, A("ER%d" % t), A("EO"), "ae%d" % t, "se%d" % t)
+        spread("P4", 256, "SELR", 0, 16, True, "RP")
+        act(A("KRW"), A("P4", 256, 512), AF.Copy)
+        act(A("KRB"), IND(A("KRW"), A("LB")), AF.Copy)
+        if t < RO - 1:
+            cp(IND(A("XW"), A("LSD")), A("XU"))
+        tt(A("OT"), A("DB"), A("P1", 256, 512), OP.mult)
+        ts(A("OHR"), A("KRB"), A("KC"), OP.is_equal)
+        tt(A("ERV"), A("OHR"), A("P1", 0, 256), OP.mult)
+        if t == RO - 1:
+            tt(IND(A("OWN"), A("LSD")), A("OT"), A("B0W"), OP.add)
+            dma("g", ext(T.yown[:]), (T.OWN[0::16, 0:S], [("OWN", 0, S)]), "d_yo")
+        cp(IND(A("ERW"), A("LBD")), A("ERV"))
+        if t < RO - 1:
+            tt(A("PW"), A("FT"), A("P1", 256, 512), OP.mult)
+        tt(A("M1"), A("MI"), A("ERW", 0, L), OP.max)
+        if t < RO - 1:
+            tt(IND(A("OWN"), A("LSD")), A("OT"), A("B0W"), OP.add)
+        tt(A("M2"), A("M1"), A("ER%d" % t), OP.max)
+        ts(A("MI"), A("M2"), 4095, OP.bitwise_and)
+        if t == RO - 1:
+            cp(A("PW"), A("MI"))
+            dma("y", ext(T.ym[:]), A("PW"), "d_ym")
+        else:
+            cp(A("ML"), A("MI"))
+            arrives("LI%d" % (t + 1), "al%d" % (t + 1), T.cores[(rank - 2 - t) % N])
+            send(T.cores[(rank + 2 + t) % N], A("LI%d" % (t + 1)), A("ML"), "al%d" % (t + 1), "sl%d" % (t + 1))
+            fill(A("ERW", 0, L), 0.0)
+    for s in SEMAPHORES:
+        if done[s]:
+            wait("g", s, done[s])

@@ -203,7 +203,6 @@ def rank_program(g, core, T, topo):
     ts(A("SMF", 0, 256), A("CM"), 0.0, OP.is_equal, BIG, OP.mult)
     ts(A("SMA"), A("CM"), 0.0, OP.not_equal)
     ts(A("DG"), A("CM"), A("KC"), OP.is_equal)
-    fill(A("ERW"), 0.0)
 
     def late_constants():
         ts(A("JC", 0, 128), A("LJT", 0, 128), 64.0, OP.mult)
@@ -230,12 +229,12 @@ def rank_program(g, core, T, topo):
                 o = A("SEL", 128 * (i + h), 128 * (i + h) + 128)
                 aff(o, o, [[0, 128]], OP.not_equal, c, -96, 1)
             sel("SELR", h, 8 * h, 1.0)
+        for r in range(16):
+            aff(A("ERC", 128 * r, 128 * r + 128), A("IDB"), [[-16, 8], [0, 16]], OP.is_equal, 0.0, -r, 1)
 
     def later_constants():
         ts(A("ALS"), A("AI0"), A("KC"), OP.add, float(S), OP.add)
         ts(A("ALB"), A("AI0"), A("KC"), OP.add, float(L + 1), OP.add)
-        for r in range(16):
-            ts(A("ERC", 128 * r, 128 * r + 128), A("IDB"), A("R16", r, r + 1), OP.mult)
         ts(A("LJT", 0, 128), A("CM", 0, 128), A("R16", 2, 3), OP.mult, 64.0, OP.mult)
         aff(A("LJT", 0, 128), A("LJT", 0, 128), [[0, 128]], OP.is_equal, 0.0, -2, 1)
         ts(A("LJT", 128, 256), A("BO"), A("R16", 1, 2), OP.mult, -1024.0, OP.mult)
@@ -268,7 +267,7 @@ def rank_program(g, core, T, topo):
         if first:
             later.append(lambda: cp(A("TE"), A("THC")))
         else:
-            later.append(lambda: cp(A("WI"), A("P3", 0, 1)))
+            later.append(lambda: cp(A("WI"), A("P6", 0, 1)))
             later.append(lambda: ts(A("WJ"), A("WI"), 4, OP.logical_shift_right, 63, OP.bitwise_and))
             later.append(lambda: tt(A("TE"), A("THC"), A("WJ"), OP.add))
         later.append(lambda: ts(A("THI"), A("TE"), 6, OP.logical_shift_right))
@@ -310,14 +309,17 @@ def rank_program(g, core, T, topo):
 
     turn = [0]
 
-    def diff(src, cen, h, b, banks):
+    def diff(src, cen, h, b, banks, hold=False):
         bank = banks[turn[0] % len(banks)]
         turn[0] += 1
         for k in range(4):
             o = A(bank, 128 * k, 128 * k + 128)
             mm(o, A("IDB"), A(src, 2048 * h + 4 * b + k, 2048 * (h + 1), 16), True, False)
             mm(o, A("IDN"), A(cen, 128 * h, 128 * h + 128), False, True)
-        act(A("DI", 2048 * h + 512 * b, 2048 * h + 512 * b + 512), A(bank), AF.Abs)
+
+        def out():
+            act(A("DI", 2048 * h + 512 * b, 2048 * h + 512 * b + 512), A(bank), AF.Abs)
+        return out if hold else out()
 
     def sum_d(bank, h, b, w, n=32):
         for k in range(4 * b, 4 * b + 4):
@@ -355,7 +357,7 @@ def rank_program(g, core, T, topo):
                 ts(A("EQ", off[c - 1], off[c - 1] + n), A("B1", 256 - n, 256), A("SC", 16 * c - 1, 16 * c), OP.is_equal)
         some(9)
 
-    THREE, TWO = ["P0", "P1", "P6"], ["P0", "P1"]
+    THREE, TWO, EB, NP = ["P0", "P1", "P6"], ["P0", "P1"], ["P0", "P1", "P2"], 3
     seq = [(h, b) for h in range(2) for b in range(4)]
     for t in range(RO):
         host = T.cores[(rank + 1 + t) % N]
@@ -363,20 +365,23 @@ def rank_program(g, core, T, topo):
         LI = "LI%d" % t
         turn[0] = 0
         for c in range(4):
-            gather("v" if t == 0 and c == 1 else "s", "GR", "ML", c)
+            gather("v" if c == 1 else "s", "GR", "ML", c)
             if t > 0 and c == 1:
                 act(A("SD"), A("PW"), AF.Copy, accum=A("WC"))
-                mm(A("P3", 0, 1), A("ONF"), A("WC"), True, True)
+                mm(A("P6", 0, 1), A("ONF"), A("WC"), True, True)
         for c in range(4):
             gather("s", "GI", LI, c)
-        for c in (1, 0, 2, 3) if t == 0 else range(4):
+        for c in (1, 0, 2, 3):
             scans("GR", c, 3)
             if c == 0:
                 if t == 0:
                     late_constants()
-                limits(t == 0)
                 six(LI)
+                if t == 0:
+                    limits(True)
         some(99)
+        if t > 0:
+            limits(False)
         centre("CR", 0, 256)
         scans("GI", 0)
         scans("GI", 1)
@@ -385,6 +390,7 @@ def rank_program(g, core, T, topo):
             mm(A(PSUM[3 + h]), A("ONE"), A("JC"), True, False)
             mm(A(PSUM[3 + h], 0, 128), A("MLO", 128 * h, 128 * h + 128), A("IDB"))
             mm(A(PSUM[3 + h], 128, 256), A("MHI", 128 * h, 128 * h + 128), A("IDB"))
+        some(2)
         scans("GI", 2)
         scans("GI", 3)
         diff("GI", "CI", 0, 0, THREE)
@@ -404,7 +410,9 @@ def rank_program(g, core, T, topo):
             scan(A("KSC", 256 * h, 256 * h + 256), A("SMF", 0, 256), A(PSUM[3 + h], 0, 256), OP.add, OP.min, BIG)
         diff("GR", "CR", 0, 0, THREE)
         turned(32, "P2", A("KSC", 15, 512, 16))
+        some(4)
         low(32, "P2", 63)
+        some(2)
         diff("GR", "CR", 0, 1, THREE)
         spread("P2", 0, "SEL", 0, 32)
         diff("GR", "CR", 0, 2, THREE)
@@ -412,6 +420,7 @@ def rank_program(g, core, T, topo):
         scan(A("SS"), A("SMA"), A("SD"), OP.mult, OP.add)
         cp(A("LS"), A("SS", 15, 256, 16))
         cp(A("NL"), IND(A("NBW"), A("LS")))
+        some(99)
         mm(A("P5", 0, 128), A("ONE"), A("JC", 256, 384), True, False)
         sum_d("P5", 0, 0, "WRD", 8)
         diff("GR", "CR", 0, 3, THREE)
@@ -439,64 +448,57 @@ def rank_program(g, core, T, topo):
         for i in range(4):
             for j in range(4):
                 mm(A(PSUM[3 + i], 128 * j, 128 * j + 128), A("MHI" if j % 2 else "MLO", 128 * (i % 2), 128 * (i % 2) + 128), A("IDB"))
-        diff("GN", "CB", 0, 0, TWO)
-        diff("GN", "CB", 0, 1, TWO)
+        for b in range(NP):
+            diff("GN", "CB", 0, b, EB)
         sum_g("P3", "GN", 0, "WER")
         same(4, 16)
-        mm(A("P2", 0, 256), A("BO"), A("EQ", 0, 256), True, False)
-        for c in range(15):
-            n = 240 - 16 * c
-            mm(A("P2", 256 - n, 256), A("BO"), A("EQ", off[c], off[c] + n), False, c == 14)
         for h in range(2):
             tt(A("DD", 64 + 8 * h, 72 + 8 * h), A("KSO", 256 * h + 15, 256 * h + 128, 16), A("KSO", 256 * h + 143, 256 * h + 256, 16), OP.subtract)
         ts(A("DBA"), A("B1"), 256.0, OP.is_equal, -256.0, OP.mult)
         for i, (h, b) in enumerate(seq):
             if i == 1:
                 sum_g("P4", "GN", 1, "WER")
-            if 0 < i < 7:
-                diff("GN", "CB", seq[i + 1][0], seq[i + 1][1], TWO)
+            if 0 < i < 9 - NP:
+                diff("GN", "CB", seq[i + NP - 1][0], seq[i + NP - 1][1], EB)
             for k in (2 * i, 2 * i + 1):
                 tt(A("MX", 256 * k, 256 * k + 256), A("GN", k, 16 * L, 16), A("P7", 256, 512), OP.max)
                 for hh in range(2):
                     sum_x(PSUM[3 + hh], hh, k, "WEX")
             sum_d(PSUM[5 + h], h, b, "WER")
-            if i == 3:
-                ts(A("NF"), A("P2", 0, 256), 1.5, OP.is_gt)
-            if i == 5:
-                for r in range(16):
-                    mm(A("P2", 256, 272), A("ERC", 128 * r, 128 * r + 128), A("NF", r, 256, 16), r == 0, r == 15)
+        held = [diff("GR", "CR", 1, b, TWO, True) for b in range(2)]
+        mm(A("P2", 0, 256), A("BO"), A("EQ", 0, 256), True, False)
+        for c in range(15):
+            n = 240 - 16 * c
+            mm(A("P2", 256 - n, 256), A("BO"), A("EQ", off[c], off[c] + n), False, c == 14)
         tt(A("SCR", 0, 16), A("ALS"), A("SS", 15, 256, 16), OP.subtract)
         tt(A("SCR", 32, 48), A("ALB"), A("SC", 15, 256, 16), OP.subtract)
-        tt(A("SCR", 16, 32), A("SCR", 0, 16), A("P2", 256, 272), OP.mult)
-        tt(A("SCR", 48, 64), A("SCR", 32, 48), A("P2", 256, 272), OP.mult)
-        tt(A("SCR", 0, 16), A("SCR", 16, 32), A("SS", 15, 256, 16), OP.add)
-        tt(A("SCR", 32, 48), A("SCR", 48, 64), A("SC", 15, 256, 16), OP.add)
-        cp(A("LSD"), A("SCR", 0, 16))
-        ts(A("LBD"), A("SCR", 32, 48), -1.0, OP.add)
-        if t < RO - 1:
-            ts(A("XU"), IND(A("XW"), A("LSD")), -float(WEAR), OP.add, 0.0, OP.max)
 
         def fam(o, bank, c):
             act(A("FAM", o, o + 128), A(bank, c, c + 128), AF.Sign, -0.5, -1.0)
 
         def key(out, h, bank):
             scan(A(out, 512 * h, 512 * h + 512), A("SMF"), A(bank), OP.add, OP.min, BIG)
+        key("EK", 0, "P5")
         fam(128, "P4", 0)
         key("EI", 0, "P3")
-        fam(0, "P3", 0)
-        key("EI", 1, "P4")
-        fam(384, "P6", 256)
-        key("EK", 0, "P5")
         fam(256, "P5", 256)
+        fam(384, "P6", 256)
+        key("EI", 1, "P4")
+        fam(0, "P3", 0)
         key("EK", 1, "P6")
         mm(A("P7", 0, 128), A("ONE"), A("JC", 256, 384), True, False)
-        for b in range(4):
+        for out in held:
+            out()
+        act(A("OT"), A("P2", 0, 256), AF.Sign, -1.5)
+        act(A("NF"), A("OT"), AF.Identity, 0.5, 0.5)
+        for b in (2, 3):
             diff("GR", "CR", 1, b, TWO)
         for b in range(4):
             sum_d("P7", 1, b, "WRD", 8)
         act(A("B0W"), A("B1"), AF.Identity, -1.0)
         act(A("DB"), A("DBA"), AF.Identity, 1.0)
         act(A("FT"), A("NF"), AF.Identity, 1.0, -1.0)
+        act(A("ERW", 0, L), A("SS"), AF.Identity, 0.0, 0.0)
         tt(A("DD", 0, 64), A("EI", 15, 1024, 16), A("EK", 15, 1024, 16), OP.subtract)
         scan(A("CUM", 16, 272), A("FAM", 0, 256), A("FAM", 256, 512), OP.add, OP.subtract)
         tt(A("SELT", 80, 96), A("CUM", 31, 272, 16), A("CUM", 15, 256, 16), OP.is_gt)
@@ -517,16 +519,24 @@ def rank_program(g, core, T, topo):
         spread("P0", 256, "SEL", 6, 97)
         spread("P1", 0, "SEL", 8, 97)
         spread("P1", 256, "SEL", 4, 97)
+        spread("P4", 256, "SELR", 0, 16, True, "RP")
+        for r in range(16):
+            mm(A("P5", 0, 16), A("ERC", 128 * r, 128 * r + 128), A("NF", r, 256, 16), r == 0, r == 15)
         ts(A("OHI"), A("P0", 0, 256), A("KC"), OP.is_equal)
         tt(A("EO"), A("OHI"), A("P0", 256, 512), OP.mult)
         arrives("ER%d" % t, "ae%d" % t, host)
         send(guest, A("ER%d" % t), A("EO"), "ae%d" % t, "se%d" % t)
-        spread("P4", 256, "SELR", 0, 16, True, "RP")
         act(A("KRW"), A("P4", 256, 512), AF.Copy)
         act(A("KRB"), IND(A("KRW"), A("LB")), AF.Copy)
-        if t < RO - 1:
-            cp(IND(A("XW"), A("LSD")), A("XU"))
+        tt(A("SCR", 16, 32), A("SCR", 0, 16), A("P5", 0, 16), OP.mult)
+        tt(A("SCR", 48, 64), A("SCR", 32, 48), A("P5", 0, 16), OP.mult)
+        tt(A("SCR", 0, 16), A("SCR", 16, 32), A("SS", 15, 256, 16), OP.add)
+        tt(A("SCR", 32, 48), A("SCR", 48, 64), A("SC", 15, 256, 16), OP.add)
+        cp(A("LSD"), A("SCR", 0, 16))
+        ts(A("LBD"), A("SCR", 32, 48), -1.0, OP.add)
         tt(A("OT"), A("DB"), A("P1", 256, 512), OP.mult)
+        if t < RO - 1:
+            act(A("XU"), IND(A("XW"), A("LSD")), AF.Relu, -float(WEAR))
         ts(A("OHR"), A("KRB"), A("KC"), OP.is_equal)
         tt(A("ERV"), A("OHR"), A("P1", 0, 256), OP.mult)
         if t == RO - 1:
@@ -537,6 +547,7 @@ def rank_program(g, core, T, topo):
             tt(A("PW"), A("FT"), A("P1", 256, 512), OP.mult)
         tt(A("M1"), A("MI"), A("ERW", 0, L), OP.max)
         if t < RO - 1:
+            cp(IND(A("XW"), A("LSD")), A("XU"))
             tt(IND(A("OWN"), A("LSD")), A("OT"), A("B0W"), OP.add)
         tt(A("M2"), A("M1"), A("ER%d" % t), OP.max)
         ts(A("MI"), A("M2"), 4095, OP.bitwise_and)
@@ -547,7 +558,6 @@ def rank_program(g, core, T, topo):
             cp(A("ML"), A("MI"))
             arrives("LI%d" % (t + 1), "al%d" % (t + 1), T.cores[(rank - 2 - t) % N])
             send(T.cores[(rank + 2 + t) % N], A("LI%d" % (t + 1)), A("ML"), "al%d" % (t + 1), "sl%d" % (t + 1))
-            fill(A("ERW", 0, L), 0.0)
     for s in SEMAPHORES:
         if done[s]:
             wait("g", s, done[s])

from concourse.mybir import AluOpType as OP, ActivationFunctionType as AF
import comms_topo

S, L, RO, WEAR = 4096, 256, 3, 8
BIG = float(2 ** 26)
B, F, I, U = "bfloat16", "float32", "int32", "uint16"
SCRATCH = {"OD": ("dram", [8, S], B)}
for _d, _l in ((B, "XW:4352 OWN:4352 GR:4096 GI:4096 GN:4096 S1:4096 S2:4096 DI:4096 MX:4096 CR:256 CI:256 CB:256 THB:128 ONE:128 IDB:128 IDN:128 "
                   "IDH:128 IDC:128 BO:128 MHALF:128 DGA:256 SM1:1024 SM2:1024 ERC:2048 WB:32 WID:32 WIX:32 WIG:32 WER:32 WEX:32 WRD:8 JC:512 LJT:256 LJ:1024 "
                   "NC:512 SEL:1280 SELR:256 MLO:256 MHI:256 TP:128 RP:128 SCM:256 SC:256 B1:256 KRW:256 KRB:256 OHR:256 EQ:2176 NF:256 FT:256 FAM:512 OHI:256 "
                   "B0W:256 DBA:256 DB:256 OT:256 XU:256"),
               (F, "EO:256 ER0:256 ER1:256 ER2:256 TA:1 TB:1 ONF:128 IDF:128 KC:1 CM:256 DG:256 SMF:512 SMA:256 R16:16 AI0:16 ALS:16 ALB:16 "
                   "KSC:512 KSO:512 KSR:256 EI:1024 EK:1024 SD:256 SS:256 SCR:64 CUM:272 DD:80 SELT:104 TS:64 ERV:256 ERW:512 PW:256 WC:1 M1:256"),
               (I, "NBW:4096 MI:256 THC:1 TE:1 THI:1 TLO:1 WI:1 WJ:1 NI:256 NJ:256 TT:128 TU:128 RT:128 RU:128 M2:256"),
               (U, "ML:256 LI0:256 LI1:256 LI2:256 LS:16 LB:16 NL:256 LSD:16 LBD:16")):
    for _e in _l.split():
        SCRATCH[_e.split(":")[0]] = ("sbuf", [128, int(_e.split(":")[1])], _d)
PSUM = ["P%d" % i for i in range(8)]
for _p in PSUM:
    SCRATCH[_p] = ("psum", [128, 512], F)
SEMAPHORES = (["q_v", "q_s", "q_t", "q_g"] + ["d_" + n for n in ("x", "m", "o", "nb", "th", "od", "ow", "ym", "yo")]
              + [n + str(t) for n in ("al", "ae", "sl", "se") for t in range(RO)])


def rank_program(g, core, T, topo):
    rank = T.rank_of(core)
    if rank is None:
        return
    N = len(T.cores)
    Q = {"v": g.vector, "s": g.scalar, "t": g.tensor, "g": g, "y": g.sync}
    done = {n: 0 for n in SEMAPHORES}
    know = {q: {} for q in Q}
    clock = {}
    acc = {}

    def A(name, c0=0, c1=None, st=1, p0=None, p1=None):
        t = T[name]
        c1 = t.shape[1] if c1 is None else c1
        ps = slice(None) if p0 is None else slice(p0, p1)
        return (t[ps, slice(c0, c1) if st == 1 else slice(c0, c1, st)], [(name, c0, c1)])

    def IND(win, off):
        return (win[0].indirect(off[0]), win[1] + off[1])

    def ext(t):
        return (t, [])

    def conflicts(q, reads, writes):
        need = {}
        for regs, wr in ((reads, False), (writes, True)):
            for (b, c0, c1) in regs:
                for (aq, aw, a0, a1, sem, val) in acc.get(b, []):
                    if b in PSUM:
                        if aq == q and (q == "t" or not aw or a1 <= c0 or a0 >= c1):
                            continue
                    elif not (aw or wr) or a1 <= c0 or a0 >= c1:
                        continue
                    need[sem] = max(need.get(sem, 0), val)
        return need

    def wait(q, sem, val):
        if know[q].get(sem, 0) >= val:
            return
        Q[q].wait_ge(T.sem[sem], val)
        for k, v in clock.get((sem, val), {}).items():
            know[q][k] = max(know[q].get(k, 0), v)
        know[q][sem] = max(know[q].get(sem, 0), val)

    def note(q, reads, writes, sem, val):
        for regs, wr in ((writes, True), (reads, False)):
            for (b, c0, c1) in regs:
                l = acc.setdefault(b, [])
                if b in PSUM:
                    l[:] = [x for x in l if x[0] == q and not (x[2] >= c0 and x[3] <= c1 and (wr or not x[1]))]
                else:
                    l[:] = [x for x in l if not (x[2] >= c0 and x[3] <= c1 and (wr or (x[0] == q and not x[1])))]
                l.append((q, wr, c0, c1, sem, val))

    def waits(q, reads, writes):
        need = conflicts(q, reads, writes)
        for s in sorted(need, key=lambda s: -sum(1 for o in need if o != s and clock.get((s, need[s]), {}).get(o, 0) >= need[o])):
            wait(q, s, need[s])

    def flat(l):
        return [r for x in l for r in x[1]]

    def emit(q, call, writes, reads, sem=None, n=1):
        reads, writes = flat(reads), flat(writes)
        waits(q, reads, writes)
        sem = sem or "q_" + q
        done[sem] += n
        call().then_inc(T.sem[sem], n)
        clock[(sem, done[sem])] = dict(know[q])
        note(q if n == 1 else "d" + sem, reads, writes, sem, done[sem])

    def w_emit(q, call, out, reads):
        emit(q, call, [(None, out[1][:1])], list(reads) + [(None, out[1][1:])])

    def cp(out, i):
        w_emit("v", lambda: g.vector.tensor_copy(out[0], i[0]), out, [i])

    def tt(out, a, b, op):
        w_emit("v", lambda: g.vector.tensor_tensor(out[0], a[0], b[0], op), out, [a, b])

    def ts(out, a, s1, op0, s2=None, op1=None):
        col = [s1] if isinstance(s1, tuple) else []
        v = s1[0] if col else s1
        if op1 is None:
            w_emit("v", lambda: g.vector.tensor_scalar(out[0], a[0], v, None, op0), out, [a] + col)
        else:
            w_emit("v", lambda: g.vector.tensor_scalar(out[0], a[0], v, s2, op0, op1), out, [a] + col)

    def scan(out, d0, d1, op0, op1, init=0.0):
        w_emit("v", lambda: g.vector.tensor_tensor_scan(out[0], d0[0], d1[0], init, op0, op1), out, [d0, d1])

    def fill(out, c):
        w_emit("v", lambda: g.vector.memset(out[0], c), out, [])

    def act(out, i, func, bias=0.0, scale=1.0, accum=None):
        emit("s", lambda: g.scalar.activation(out[0], i[0], func, bias=bias, scale=scale, accum_out=accum and accum[0]), [out] + ([accum] if accum else []), [i])

    def mm(out, l, r, start=False, stop=False):
        emit("t", lambda: g.tensor.matmul(out[0], l[0], r[0], start, stop), [out], [l, r])

    def aff(out, i, pat, op, fl, base, cm):
        emit("g", lambda: g.affine_select(out[0], i[0], pat, op, fl, base, cm), [out], [i])

    def iota(out, pat, cm):
        emit("g", lambda: g.iota(out[0], pat, 0, cm, allow_small_or_imprecise_dtypes=True), [out], [])

    def dma(q, out, i, sem):
        emit(q, lambda: Q[q].dma_start(out[0], i[0]), [out], [i], sem, 16)

    def dmas(q, calls, out, i, sem):
        waits(q, flat(i), out[1])
        for call in calls:
            call().then_inc(T.sem[sem], 16)
        done[sem] += 16 * len(calls)
        clock[(sem, done[sem])] = dict(know[q])
        note("d" + sem, flat(i), out[1], sem, done[sem])

    def lanes(src, dst):
        return topo.engines(src, dst)[:8]

    def send(dst, out, i, rsem, lsem):
        rid, pid = topo.addr(dst)[:2]
        eng = lanes(core, dst)
        waits("g", i[1], [])
        g.remote_dma(out[0], i[0], T.sem[rsem], T.sem[lsem], pid, rid, sum(1 << e for e in eng))
        done[lsem] += len(eng)
        clock[(lsem, done[lsem])] = dict(know["g"])
        note("r" + lsem, i[1], [], lsem, done[lsem])

    def arrives(name, rsem, src):
        done[rsem] += len(lanes(src, core))
        note("n" + rsem, [], A(name)[1], rsem, done[rsem])

    fill(A("THC"), 0)
    dma("y", A("XW", 0, S), ext(T.x0[:]), "d_x")
    dma("s", A("MI"), ext(T.m0[:]), "d_m")
    dma("s", A("NI"), ext(T.own0[:]), "d_o")
    dmas("y", [lambda r=r: g.sync.dma_start(T.THC[r::16, 0:1], T.th[:]) for r in range(2)], A("THC"), [], "d_th")
    dma("y", A("NBW"), ext(T.nb[:]), "d_nb")
    fill(A("ONE"), 1.0)
    iota(A("CM"), [[0, 16], [1, 16]], 0)
    iota(A("WI"), [[0, 1]], 1)
    aff(A("IDB"), A("ONE"), [[-1, 128]], OP.is_equal, 0.0, 0, 1)
    aff(A("WB"), A("ONE", 0, 32), [[0, 4], [-16, 8]], OP.is_ge, 0.0, 0, 1)
    aff(A("WB"), A("WB"), [[0, 4], [16, 8]], OP.is_ge, 0.0, 15, -1)
    aff(A("BO"), A("ONE"), [[-16, 8], [0, 16]], OP.is_ge, 0.0, 0, 1)
    aff(A("BO"), A("BO"), [[16, 8], [0, 16]], OP.is_ge, 0.0, 15, -1)
    iota(A("AI0"), [[16, 16]], 0)
    fill(A("MHALF"), -0.5)
    ts(A("SM1", 0, 256), A("CM"), 0.0, OP.not_equal)
    ts(A("SM2", 0, 256), A("CM"), 0.0, OP.is_equal, 1024.0, OP.mult)
    for c in (256, 512):
        for n in ("SM1", "SM2"):
            cp(A(n, c, 2 * c), A(n, 0, c))
    ts(A("WJ"), A("WI"), 15, OP.bitwise_and)
    ts(A("IDH"), A("IDB"), 0.5, OP.mult)
    cp(A("KC"), A("WJ"))
    cp(A("ML"), A("MI"))
    arrives("LI0", "al0", T.cores[(rank - 1) % N])
    send(T.cores[(rank + 1) % N], A("LI0"), A("ML"), "al0", "sl0")
    cp(A("CB"), A("NI"))
    dma("y", (T.OD[:], [("OD", 0, S)]), A("CB"), "d_od")
    dmas("y", [lambda r=r: g.sync.dma_start(T.OWN[r::16, 0:S], T.OD[:]) for r in range(16)], A("OWN", 0, S), [("", [("OD", 0, S)])], "d_ow")
    ts(A("IDN"), A("IDB"), -1.0, OP.mult)
    ts(A("WID", 0, 16), A("WB", 0, 16), 1024.0, OP.mult)
    ts(A("WID", 16, 24), A("WB", 0, 8), -64.0, OP.mult)
    ts(A("WID", 24, 32), A("WB", 0, 8), 64.0, OP.mult)
    ts(A("WER", 0, 16), A("WB", 0, 16), -1024.0, OP.mult)
    ts(A("WER", 16, 32), A("WB", 0, 16), 1024.0, OP.mult)
    ts(A("WRD"), A("WB", 0, 8), -64.0, OP.mult)
    ts(A("WIX"), A("WID"), 2.0, OP.mult)
    ts(A("WIG"), A("WID"), -1.0, OP.mult)
    ts(A("WEX"), A("WER"), -2.0, OP.mult)
    fill(A("SEL"), 0.0)
    fill(A("SELR"), 0.0)
    ts(A("R16"), A("CM", 0, 16), A("KC"), OP.is_equal)
    ts(A("LJT", 0, 128), A("CM", 0, 128), A("R16", 0, 1), OP.mult)
    aff(A("LJT", 0, 128), A("LJT", 0, 128), [[0, 128]], OP.is_equal, 0.0, 0, 1)
    ts(A("SMF", 0, 256), A("CM"), 0.0, OP.is_equal, BIG, OP.mult)
    ts(A("SMA"), A("CM"), 0.0, OP.not_equal)
    ts(A("DG"), A("CM"), A("KC"), OP.is_equal)

    def late_constants():
        ts(A("JC", 0, 128), A("LJT", 0, 128), 64.0, OP.mult)
        ts(A("JC", 128, 256), A("LJT", 0, 128), 64.0, OP.mult)
        cp(A("JC", 256, 384), A("LJT", 0, 128))
        cp(A("JC", 384, 512), A("LJT", 0, 128))
        cp(A("IDF"), A("IDB"))
        ts(A("DGA"), A("DG"), 1001.0, OP.mult, -1000.0, OP.add)

        def sel(name, i, row, weight):
            o = A(name, 128 * i, 128 * i + 128)
            aff(o, o, [[-1, 8], [0, 16]], OP.not_equal, weight, -row, 1)
        for h in range(2):
            sel("SEL", h, 16 * h, 1.0)
            sel("SEL", h, 16 * h + 8, 64.0)
        for h in range(2):
            sel("SEL", 2 + h, 64 + 8 * h, 1.0)
            sel("SEL", 4 + h, 80 + 8 * h, 1.0)
            sel("SEL", 6 + h, 32 * h, 1.0)
            sel("SEL", 6 + h, 32 * h + 8, 64.0)
            sel("SEL", 8 + h, 32 * h + 16, 1.0)
            sel("SEL", 8 + h, 32 * h + 24, 64.0)
            for i, c in ((6, 8192.0), (8, 4096.0)):
                o = A("SEL", 128 * (i + h), 128 * (i + h) + 128)
                aff(o, o, [[0, 128]], OP.not_equal, c, -96, 1)
            sel("SELR", h, 8 * h, 1.0)
        for r in range(16):
            aff(A("ERC", 128 * r, 128 * r + 128), A("IDB"), [[-16, 8], [0, 16]], OP.is_equal, 0.0, -r, 1)

    def later_constants():
        ts(A("ALS"), A("AI0"), A("KC"), OP.add, float(S), OP.add)
        ts(A("ALB"), A("AI0"), A("KC"), OP.add, float(L + 1), OP.add)
        ts(A("LJT", 0, 128), A("CM", 0, 128), A("R16", 2, 3), OP.mult, 64.0, OP.mult)
        aff(A("LJT", 0, 128), A("LJT", 0, 128), [[0, 128]], OP.is_equal, 0.0, -2, 1)
        ts(A("LJT", 128, 256), A("BO"), A("R16", 1, 2), OP.mult, -1024.0, OP.mult)
        for i in range(2):
            ts(A("NC", 128 * i, 128 * i + 128), A("BO"), -1024.0, OP.mult)
            ts(A("NC", 128 * i + 256, 128 * i + 384), A("BO"), 1024.0, OP.mult)
        ts(A("IDC"), A("IDB"), 100.0, OP.mult)
        fill(A("ONF"), 1.0)
        fill(A("XW", S, S + L), 0.0)
        fill(A("OWN", S, S + L), 0.0)
        fill(A("CUM", 0, 16), 0.0)
        fill(A("SELT"), 1.0)
        tt(A("LJT", 128, 256), A("LJT", 128, 256), A("LJT", 0, 128), OP.add)
        for i in range(8):
            c = 128 * i
            if i in (0, 6):
                ts(A("LJ", c, c + 128), A("BO"), A("R16", 0, 1), OP.mult, -65536.0, OP.mult)
                tt(A("LJ", c, c + 128), A("LJ", c, c + 128), A("LJT", 128, 256), OP.add)
            else:
                cp(A("LJ", c, c + 128), A("LJT", 0, 128))
        cp(A("SMF", 256, 512), A("SMF", 0, 256))

    later = []

    def some(n):
        for _ in range(min(n, len(later))):
            later.pop(0)()

    def limits(first):
        if first:
            later.append(lambda: cp(A("TE"), A("THC")))
        else:
            later.append(lambda: cp(A("WI"), A("P6", 0, 1)))
            later.append(lambda: ts(A("WJ"), A("WI"), 4, OP.logical_shift_right, 63, OP.bitwise_and))
            later.append(lambda: tt(A("TE"), A("THC"), A("WJ"), OP.add))
        later.append(lambda: ts(A("THI"), A("TE"), 6, OP.logical_shift_right))
        later.append(lambda: ts(A("TLO"), A("TE"), 63, OP.bitwise_and))
        later.append(lambda: tt(A("TA"), A("THI"), A("R16", 0, 1), OP.mult))
        later.append(lambda: tt(A("TB"), A("TLO"), A("R16", 1, 2), OP.mult))
        later.append(lambda: tt(A("TA"), A("TA"), A("TB"), OP.add))
        later.append(lambda: tt(A("TB"), A("TA"), A("R16", 2, 3), OP.add))
        later.append(lambda: ts(A("THB"), A("ONE"), A("TB"), OP.mult))

    def six(lst):
        later.append(lambda: cp(A("NI"), A(lst)))
        later.append(lambda: ts(A("NJ"), A("NI"), 63, OP.bitwise_and))
        later.append(lambda: ts(A("M2"), A("NI"), 6, OP.logical_shift_right))
        later.append(lambda: cp(A("MLO"), A("NJ")))
        later.append(lambda: cp(A("MHI"), A("M2")))

    def gather(q, dst, lst, c):
        out, src = A(dst, 1024 * c, 1024 * c + 1024), IND(A("XW", 0, S), A(lst, 64 * c, 64 * c + 64))
        if q == "v":
            cp(out, src)
        else:
            act(out, src, AF.Copy)

    def scans(src, c, n=0):
        o = 1024 * c
        scan(A("S1", o, o + 1024), A("SM1"), A(src, o, o + 1024), OP.mult, OP.max)
        some(n)
        scan(A("S2", o, o + 1024), A("SM2"), A(src, o, o + 1024), OP.add, OP.min, BIG)
        some(n)

    def centre(dst, a0, n):
        for a in range(a0, a0 + n, 128):
            p = A("P2", a - a0, a - a0 + 128)
            mm(p, A("IDH"), A("S1", 16 * a + 15, 16 * a + 2048, 16), True, False)
            mm(p, A("IDH"), A("S2", 16 * a + 15, 16 * a + 2048, 16))
            mm(p, A("IDH"), A("MHALF"), False, True)
        ts(A(dst, a0, a0 + n), A("P2", 0, n), float(2 ** 23), OP.add, -float(2 ** 23), OP.add)

    turn = [0]

    def diff(src, cen, h, b, banks, hold=False):
        bank = banks[turn[0] % len(banks)]
        turn[0] += 1
        for k in range(4):
            o = A(bank, 128 * k, 128 * k + 128)
            mm(o, A("IDB"), A(src, 2048 * h + 4 * b + k, 2048 * (h + 1), 16), True, False)
            mm(o, A("IDN"), A(cen, 128 * h, 128 * h + 128), False, True)

        def out():
            act(A("DI", 2048 * h + 512 * b, 2048 * h + 512 * b + 512), A(bank), AF.Abs)
        return out if hold else out()

    def sum_d(bank, h, b, w, n=32):
        for k in range(4 * b, 4 * b + 4):
            mm(A(bank, k, 16 * n, 16), A("DI", 2048 * h + 128 * k, 2048 * h + 128 * k + 128), A(w), False, k == 15)

    def sum_g(bank, src, h, w):
        for k in range(16):
            mm(A(bank, k, 512, 16), A(src, 2048 * h + k, 2048 * (h + 1), 16), A(w))

    def sum_x(bank, h, k, w):
        mm(A(bank, k, 512, 16), A("MX", 256 * k + 128 * h, 256 * k + 128 * h + 128), A(w), False, k == 15)

    def turned(n, bank, src):
        o = A(bank, 0, 128, 1, 0, n)
        emit("t", lambda: g.tensor.transpose(o[0], src[0], A("IDF")[0]), [o], [src, A("IDF")])

    def low(n, bank, mask, x="T"):
        cp(A(x + "T", 0, 128, 1, 0, n), A(bank, 0, 128, 1, 0, n))
        ts(A(x + "U", 0, 128, 1, 0, n), A(x + "T", 0, 128, 1, 0, n), mask, OP.bitwise_and)
        cp(A(x + "P", 0, 128, 1, 0, n), A(x + "U", 0, 128, 1, 0, n))

    def spread(bank, o, name, i, n, start=True, x="TP"):
        for h in range(2):
            mm(A(bank, o + 128 * h, o + 128 * h + 128), A(name, 128 * (i + h), 128 * (i + h) + 128, 1, 0, n), A(x, 0, 128, 1, 0, n), start, start or h == 1)

    off = [256 + sum(240 - 16 * d for d in range(c)) for c in range(15)]

    def same(c0, c1):
        for c in range(c0, c1):
            some(1)
            if c == 0:
                tt(A("EQ", 0, 256), A("SC"), A("B1"), OP.is_equal)
            else:
                n = 256 - 16 * c
                ts(A("EQ", off[c - 1], off[c - 1] + n), A("B1", 256 - n, 256), A("SC", 16 * c - 1, 16 * c), OP.is_equal)
        some(9)

    THREE, TWO, EB, NP = ["P0", "P1", "P6"], ["P0", "P1"], ["P0", "P1", "P2"], 3
    seq = [(h, b) for h in range(2) for b in range(4)]
    for t in range(RO):
        host = T.cores[(rank + 1 + t) % N]
        guest = T.cores[(rank - 1 - t) % N]
        LI = "LI%d" % t
        turn[0] = 0
        for c in range(4):
            gather("v" if c == 1 else "s", "GR", "ML", c)
            if t > 0 and c == 1:
                act(A("SD"), A("PW"), AF.Copy, accum=A("WC"))
                mm(A("P6", 0, 1), A("ONF"), A("WC"), True, True)
        for c in range(4):
            gather("s", "GI", LI, c)
        for c in (1, 0, 2, 3):
            scans("GR", c, 3)
            if c == 0:
                if t == 0:
                    late_constants()
                six(LI)
                if t == 0:
                    limits(True)
        some(99)
        if t > 0:
            limits(False)
        centre("CR", 0, 256)
        scans("GI", 0)
        scans("GI", 1)
        centre("CI", 0, 128)
        for h in range(2):
            mm(A(PSUM[3 + h]), A("ONE"), A("JC"), True, False)
            mm(A(PSUM[3 + h], 0, 128), A("MLO", 128 * h, 128 * h + 128), A("IDB"))
            mm(A(PSUM[3 + h], 128, 256), A("MHI", 128 * h, 128 * h + 128), A("IDB"))
        some(2)
        scans("GI", 2)
        scans("GI", 3)
        diff("GI", "CI", 0, 0, THREE)
        diff("GI", "CI", 0, 1, THREE)
        diff("GI", "CI", 0, 2, THREE)
        centre("CI", 128, 128)
        mm(A("P7", 0, 128), A("IDB"), A("CI", 128, 256), True, True)
        diff("GI", "CI", 0, 3, THREE)
        sum_g("P4", "GI", 1, "WIG")
        for k in range(16):
            tt(A("MX", 256 * k + 128, 256 * k + 256), A("GI", 2048 + k, 4096, 16), A("P7", 0, 128), OP.max)
        for b in range(4):
            sum_d("P3", 0, b, "WID")
            for k in range(4 * b, 4 * b + 4):
                sum_x("P4", 1, k, "WIX")
        for h in range(2):
            scan(A("KSC", 256 * h, 256 * h + 256), A("SMF", 0, 256), A(PSUM[3 + h], 0, 256), OP.add, OP.min, BIG)
        diff("GR", "CR", 0, 0, THREE)
        turned(32, "P2", A("KSC", 15, 512, 16))
        some(4)
        low(32, "P2", 63)
        some(2)
        diff("GR", "CR", 0, 1, THREE)
        spread("P2", 0, "SEL", 0, 32)
        diff("GR", "CR", 0, 2, THREE)
        tt(A("SD"), A("P2", 0, 256), A("DG"), OP.mult)
        scan(A("SS"), A("SMA"), A("SD"), OP.mult, OP.add)
        cp(A("LS"), A("SS", 15, 256, 16))
        cp(A("NL"), IND(A("NBW"), A("LS")))
        some(99)
        mm(A("P5", 0, 128), A("ONE"), A("JC", 256, 384), True, False)
        sum_d("P5", 0, 0, "WRD", 8)
        diff("GR", "CR", 0, 3, THREE)
        for b in range(1, 4):
            sum_d("P5", 0, b, "WRD", 8)
        for c in range(4):
            gather("s", "GN", "NL", c)
        tt(A("SCM"), IND(A("OWN", 0, S), A("LS")), A("DGA"), OP.add)
        ts(A("B1"), IND(A("OWN", 0, S), A("LS")), 1.0, OP.add)
        scan(A("KSO", 0, 256), A("SMF", 0, 256), A("P3", 256, 512), OP.add, OP.min, BIG)
        scan(A("SC"), A("SM1", 0, 256), A("SCM"), OP.mult, OP.max)
        scan(A("KSO", 256, 512), A("SMF", 0, 256), A("P4", 256, 512), OP.add, OP.min, BIG)
        ts(A("LB"), A("SC", 15, 256, 16), -1.0, OP.add)
        scan(A("KSR", 0, 128), A("SMF", 0, 128), A("P5", 0, 128), OP.add, OP.min, BIG)
        cp(A("CB"), IND(A("CR"), A("LB")))
        mm(A("P7", 256, 512), A("IDB"), A("CI"), True, True)
        if t == 0:
            later_constants()
        for i in range(4):
            mm(A(PSUM[3 + i]), A("THB"), A("LJ", 512 * (i // 2), 512 * (i // 2) + 512), True, False)
            if i < 2:
                mm(A(PSUM[3 + i]), A("CI", 128 * i, 128 * i + 128), A("NC"))
        six("NL")
        same(0, 4)
        for i in range(4):
            for j in range(4):
                mm(A(PSUM[3 + i], 128 * j, 128 * j + 128), A("MHI" if j % 2 else "MLO", 128 * (i % 2), 128 * (i % 2) + 128), A("IDB"))
        for b in range(NP):
            diff("GN", "CB", 0, b, EB)
        sum_g("P3", "GN", 0, "WER")
        same(4, 16)
        for h in range(2):
            tt(A("DD", 64 + 8 * h, 72 + 8 * h), A("KSO", 256 * h + 15, 256 * h + 128, 16), A("KSO", 256 * h + 143, 256 * h + 256, 16), OP.subtract)
        ts(A("DBA"), A("B1"), 256.0, OP.is_equal, -256.0, OP.mult)
        for i, (h, b) in enumerate(seq):
            if i == 1:
                sum_g("P4", "GN", 1, "WER")
            if 0 < i < 9 - NP:
                diff("GN", "CB", seq[i + NP - 1][0], seq[i + NP - 1][1], EB)
            for k in (2 * i, 2 * i + 1):
                tt(A("MX", 256 * k, 256 * k + 256), A("GN", k, 16 * L, 16), A("P7", 256, 512), OP.max)
                for hh in range(2):
                    sum_x(PSUM[3 + hh], hh, k, "WEX")
            sum_d(PSUM[5 + h], h, b, "WER")
        held = [diff("GR", "CR", 1, b, TWO, True) for b in range(2)]
        mm(A("P2", 0, 256), A("BO"), A("EQ", 0, 256), True, False)
        for c in range(15):
            n = 240 - 16 * c
            mm(A("P2", 256 - n, 256), A("BO"), A("EQ", off[c], off[c] + n), False, c == 14)
        tt(A("SCR", 0, 16), A("ALS"), A("SS", 15, 256, 16), OP.subtract)
        tt(A("SCR", 32, 48), A("ALB"), A("SC", 15, 256, 16), OP.subtract)

        def fam(o, bank, c):
            act(A("FAM", o, o + 128), A(bank, c, c + 128), AF.Sign, -0.5, -1.0)

        def key(out, h, bank):
            scan(A(out, 512 * h, 512 * h + 512), A("SMF"), A(bank), OP.add, OP.min, BIG)
        key("EK", 0, "P5")
        fam(128, "P4", 0)
        key("EI", 0, "P3")
        fam(256, "P5", 256)
        fam(384, "P6", 256)
        key("EI", 1, "P4")
        fam(0, "P3", 0)
        key("EK", 1, "P6")
        mm(A("P7", 0, 128), A("ONE"), A("JC", 256, 384), True, False)
        for out in held:
            out()
        act(A("OT"), A("P2", 0, 256), AF.Sign, -1.5)
        act(A("NF"), A("OT"), AF.Identity, 0.5, 0.5)
        for b in (2, 3):
            diff("GR", "CR", 1, b, TWO)
        for b in range(4):
            sum_d("P7", 1, b, "WRD", 8)
        act(A("B0W"), A("B1"), AF.Identity, -1.0)
        act(A("DB"), A("DBA"), AF.Identity, 1.0)
        act(A("FT"), A("NF"), AF.Identity, 1.0, -1.0)
        act(A("ERW", 0, L), A("SS"), AF.Identity, 0.0, 0.0)
        tt(A("DD", 0, 64), A("EI", 15, 1024, 16), A("EK", 15, 1024, 16), OP.subtract)
        scan(A("CUM", 16, 272), A("FAM", 0, 256), A("FAM", 256, 512), OP.add, OP.subtract)
        tt(A("SELT", 80, 96), A("CUM", 31, 272, 16), A("CUM", 15, 256, 16), OP.is_gt)
        for h in range(2):
            for c in range(32 * h, 32 * h + 32, 8):
                tt(A("TS", c, c + 8), A("DD", c, c + 8), A("SELT", 80 + 8 * h, 88 + 8 * h), OP.mult)
        tt(A("DD", 64, 80), A("DD", 64, 80), A("SELT", 80, 96), OP.mult)
        tt(A("SELT", 0, 64), A("TS"), A("EK", 15, 1024, 16), OP.add)
        for h in range(2):
            tt(A("SELT", 64 + 8 * h, 72 + 8 * h), A("DD", 64 + 8 * h, 72 + 8 * h), A("KSO", 256 * h + 143, 256 * h + 256, 16), OP.add)
        turned(97, "P2", A("SELT", 0, 97))
        scan(A("KSR", 128, 256), A("SMF", 0, 128), A("P7", 0, 128), OP.add, OP.min, BIG)
        turned(16, "P4", A("KSR", 15, 256, 16))
        low(97, "P2", 63)
        low(16, "P4", 15, "R")
        mm(A("P0", 0, 256), A("IDC"), A("NF"), True, False)
        spread("P0", 0, "SEL", 2, 97, False)
        spread("P0", 256, "SEL", 6, 97)
        spread("P1", 0, "SEL", 8, 97)
        spread("P1", 256, "SEL", 4, 97)
        spread("P4", 256, "SELR", 0, 16, True, "RP")
        for r in range(16):
            mm(A("P5", 0, 16), A("ERC", 128 * r, 128 * r + 128), A("NF", r, 256, 16), r == 0, r == 15)
        ts(A("OHI"), A("P0", 0, 256), A("KC"), OP.is_equal)
        tt(A("EO"), A("OHI"), A("P0", 256, 512), OP.mult)
        arrives("ER%d" % t, "ae%d" % t, host)
        send(guest, A("ER%d" % t), A("EO"), "ae%d" % t, "se%d" % t)
        act(A("KRW"), A("P4", 256, 512), AF.Copy)
        act(A("KRB"), IND(A("KRW"), A("LB")), AF.Copy)
        tt(A("SCR", 16, 32), A("SCR", 0, 16), A("P5", 0, 16), OP.mult)
        tt(A("SCR", 48, 64), A("SCR", 32, 48), A("P5", 0, 16), OP.mult)
        tt(A("SCR", 0, 16), A("SCR", 16, 32), A("SS", 15, 256, 16), OP.add)
        tt(A("SCR", 32, 48), A("SCR", 48, 64), A("SC", 15, 256, 16), OP.add)
        cp(A("LSD"), A("SCR", 0, 16))
        ts(A("LBD"), A("SCR", 32, 48), -1.0, OP.add)
        tt(A("OT"), A("DB"), A("P1", 256, 512), OP.mult)
        if t < RO - 1:
            act(A("XU"), IND(A("XW"), A("LSD")), AF.Relu, -float(WEAR))
        ts(A("OHR"), A("KRB"), A("KC"), OP.is_equal)
        tt(A("ERV"), A("OHR"), A("P1", 0, 256), OP.mult)
        if t == RO - 1:
            tt(IND(A("OWN"), A("LSD")), A("OT"), A("B0W"), OP.add)
            dma("g", ext(T.yown[:]), (T.OWN[0::16, 0:S], [("OWN", 0, S)]), "d_yo")
        cp(IND(A("ERW"), A("LBD")), A("ERV"))
        if t < RO - 1:
            tt(A("PW"), A("FT"), A("P1", 256, 512), OP.mult)
        tt(A("M1"), A("MI"), A("ERW", 0, L), OP.max)
        if t < RO - 1:
            cp(IND(A("XW"), A("LSD")), A("XU"))
            tt(IND(A("OWN"), A("LSD")), A("OT"), A("B0W"), OP.add)
        tt(A("M2"), A("M1"), A("ER%d" % t), OP.max)
        ts(A("MI"), A("M2"), 4095, OP.bitwise_and)
        if t == RO - 1:
            cp(A("PW"), A("MI"))
            dma("y", ext(T.ym[:]), A("PW"), "d_ym")
        else:
            cp(A("ML"), A("MI"))
            arrives("LI%d" % (t + 1), "al%d" % (t + 1), T.cores[(rank - 2 - t) % N])
            send(T.cores[(rank + 2 + t) % N], A("LI%d" % (t + 1)), A("ML"), "al%d" % (t + 1), "sl%d" % (t + 1))
    for s in SEMAPHORES:
        if done[s]:
            wait("g", s, done[s])
